import numpy as np
import ml_dtypes


def mxq(x, axis, fmt="e4m3"):
    dtype, down = {"e4m3": (ml_dtypes.float8_e4m3fn, 7), "e5m2": (ml_dtypes.float8_e5m2, 14)}[fmt]
    v = np.moveaxis(np.asarray(x, np.float32).astype(ml_dtypes.bfloat16).astype(np.float64), axis, -1)
    blocks = v.reshape(v.shape[:-1] + (-1, 32))
    amax = np.abs(blocks).max(-1, keepdims=True)
    byte = np.maximum(np.where(amax > 0, np.frexp(amax)[1] - 1 + 127, 0) - down, 1)
    scale = np.exp2(byte - 127.0)
    codes = (blocks / scale).astype(np.float32).astype(dtype).astype(np.float64)
    return np.moveaxis((codes * scale).reshape(v.shape), -1, axis)


WIDE = False


def mx_kscale(k):
    if not WIDE:
        return np.ones(k)
    levels = np.array([10, -10, 5, -5, 0])
    if k % 512:
        return np.exp2(np.random.permutation(np.resize(levels, k // 32))).repeat(32)
    a = np.empty((k // 512, 16))
    for p in range(k // 512):
        a[p, :8] = np.random.permutation(np.resize(levels, 8))
        for g in range(8):
            far = levels[np.abs(levels - a[p, g]) >= 10]
            a[p, g + 8] = far[np.random.randint(len(far))]
    return np.exp2(a.ravel()).repeat(32)


def f64(x):
    return np.asarray(x).astype(np.float64)


def striped(idx):
    return np.tile(idx.reshape(-1, 16).T, (8, 1)).astype(np.uint16)


def unstriped(offs):
    return offs[:16].T.reshape(-1).astype(np.int64)


def pack_weight(w):
    k, n = w.shape
    w = f64(np.asarray(w, np.float32).astype(ml_dtypes.bfloat16)).reshape(k // 32, 32, n)
    amax = np.abs(w).max(1)
    byte = np.clip(np.where(amax > 0, np.frexp(amax)[1] - 1 + 127 - 7, 1), 1, 254)
    scaled = (w * np.exp2(127.0 - byte)[:, None, :]).reshape(k, n).astype(np.float32)
    words = np.ascontiguousarray(scaled.reshape(k // 512, 128, 4, n).transpose(0, 1, 3, 2)).astype(ml_dtypes.float8_e4m3fn).view(np.uint8)
    return words, np.ascontiguousarray(byte.astype(np.uint8).reshape(k // 512, 16, n))


def unpack_weight(words, scales):
    g, p, n, _ = words.shape
    vals = np.ascontiguousarray(words).view(ml_dtypes.float8_e4m3fn).astype(np.float64) * np.repeat(np.exp2(scales.astype(np.float64) - 127.0), 8, axis=1)[..., None]
    return vals.transpose(0, 1, 3, 2).reshape(g * 512, n)


K, T, S, H, V, W = 512, 1024, 512, 512, 512, 2048
P = 2 ** 7


def setup_inputs():
    n = np.random.standard_normal
    s = mx_kscale(K)[:, None]
    u = mx_kscale(H)
    packed_xT = pack_weight(n((K, T)) * s)
    packed_eT = pack_weight(n((H, W)) / np.sqrt(H) / u[:, None])
    return {
        "x_words": packed_xT[0],
        "x_scales": packed_xT[1],
        "w1": (n((K, H)) / np.sqrt(K) / s * u).astype(np.float32),
        "e_words": packed_eT[0],
        "e_scales": packed_eT[1],
        "nn": (np.tile(np.random.uniform(1.5, 3.0, W), (P, 1))).astype(np.float32),
        "own": (np.random.uniform(1.5, 3.0, (S, 1))).astype(np.float32),
        "loc": (np.tile(np.random.uniform(0.3, 1.2, W), (P, 1))).astype(np.float32),
        "iloc": (np.random.uniform(0.3, 0.8, (S, 1))).astype(np.float32),
        "offs": striped(np.random.permutation(T)[:S]),
        "anc": striped(np.random.permutation(W)[:V]),
    }


def reference(x_words, x_scales, w1, e_words, e_scales, nn, own, loc, iloc, offs, anc):
    xq = unpack_weight(x_words, x_scales)[:, unstriped(offs)]
    h = mxq(f64(w1), 0, "e4m3").T @ xq
    e_anc = unpack_weight(e_words, e_scales)[:, unstriped(anc)]
    y = mxq(h, 0, "e4m3").T @ e_anc
    dsq = f64(nn)[:1][:, unstriped(anc)] - (0.6 * y) + f64(own)
    aff = np.exp(-1.0 * (f64(iloc) * (dsq * (f64(loc)[:1][:, unstriped(anc)]))))
    deg = aff.sum(axis=1, keepdims=True) + 0.5
    return 100.0 * (aff / deg)

@@ -1,0 +1,180 @@
+from contextlib import ExitStack
+
+import concourse.mybir as mybir
+from concourse.masks import make_identity
+
+F32 = mybir.dt.float32
+BF16 = mybir.dt.bfloat16
+I32 = mybir.dt.int32
+U32 = mybir.dt.uint32
+U16 = mybir.dt.uint16
+U8 = mybir.dt.uint8
+FP8X4 = mybir.dt.float8_e4m3fn_x4
+ALU = mybir.AluOpType
+ACT = mybir.ActivationFunctionType
+
+P = 128
+PACK = 4
+K = 512
+H = 512
+S = 512
+V = 512
+T = 1024
+W = 2048
+TILES = S // P
+FLOPS = 2 * K * H * S + 2 * H * S * V
+
+
+def tile_picked_ylocsc_norm_p_kernel(
+    tc, x_words, x_scales, w1, e_words, e_scales, nn, own, loc, iloc, offs, anc, out
+):
+    nc = tc.nc
+    with ExitStack() as ctx:
+        keep = ctx.enter_context(tc.tile_pool(name="keep", bufs=1))
+        ring = ctx.enter_context(tc.tile_pool(name="ring", bufs=4))
+        once = ctx.enter_context(tc.psum_pool(name="once", bufs=1))
+        h_banks = ctx.enter_context(tc.psum_pool(name="h_banks", bufs=2))
+        y_banks = ctx.enter_context(tc.psum_pool(name="y_banks", bufs=3))
+
+        offs_t = keep.tile([P, S // 16], U16, name="offs_t")
+        anc_t = keep.tile([P, V // 16], U16, name="anc_t")
+        xw_tab = keep.tile([P, T], U32, name="xw_tab", align_bytes=64)
+        xs_tab = keep.tile([P, T], U8, name="xs_tab", align_bytes=64)
+        ew_tab = keep.tile([P, W], U32, name="ew_tab", tag="e_then_h", align_bytes=64)
+        es_tab = keep.tile([P, W], U8, name="es_tab", align_bytes=64)
+        nl_tab = keep.tile([P, W], F32, name="nl_tab", tag="nl_then_w", align_bytes=64)
+        w_raw = [keep.tile([P, PACK, H // 2], F32, name="w_raw%d" % u, align_bytes=64) for u in range(2)]
+        own_t = keep.tile([P, TILES], F32, name="own_t")
+        iloc_t = keep.tile([P, TILES], F32, name="iloc_t")
+        warm = keep.tile([P, 1], F32, name="warm")
+        warm_out = keep.tile([P, 1], F32, name="warm_out")
+        ident = keep.tile([P, P], F32, name="ident")
+
+        nc.vector.memset(xs_tab[:].bitcast(I32), 0)
+        nc.vector.memset(warm[:], 0.0)
+        nc.vector.memset(nl_tab[:], 0.0)
+        nc.vector.memset(es_tab[:].bitcast(I32), 0)
+        nc.scalar.activation(warm_out[:], warm[:], ACT.Exp)
+        make_identity(nc, ident[:])
+
+        def load_scales(table, scales):
+            for q in range(4):
+                nc.sync.dma_start(
+                    out=table[32 * q : 32 * q + 4, :].bitcast(I32), in_=scales[0, 4 * q : 4 * q + 4, :].bitcast(I32)
+                )
+
+        w_rows = w1.rearrange("(p j) c -> p j c", j=PACK)
+        nc.sync.dma_start(out=w_raw[0][:], in_=w_rows[:, :, 0 : H // 2])
+        nc.sync.dma_start(offs_t[:], offs)
+        load_scales(xs_tab, x_scales)
+        nc.sync.dma_start(anc_t[:], anc)
+        nc.sync.dma_start(out=w_raw[1][:], in_=w_rows[:, :, H // 2 : H])
+        nc.sync.dma_start(out=nl_tab[0:1, :], in_=nn[0:1, :])
+        nc.sync.dma_start(out=nl_tab[1:2, :], in_=loc[0:1, :])
+        nc.sync.dma_start(out=xw_tab[:].bitcast(I32), in_=x_words[0].rearrange("p n t -> p (n t)").bitcast(I32))
+        load_scales(es_tab, e_scales)
+        nc.sync.dma_start(out=ew_tab[:].bitcast(I32), in_=e_words[0].rearrange("p n t -> p (n t)").bitcast(I32))
+        with nc.allow_non_contiguous_dma(reason="one value a partition"):
+            nc.sync.dma_start(out=own_t[:], in_=own.rearrange("(i p) o -> p (i o)", p=P))
+            nc.sync.dma_start(out=iloc_t[:], in_=iloc.rearrange("(i p) o -> p (i o)", p=P))
+
+        xs = keep.tile([P, S], U8, name="xs", align_bytes=64)
+        nc.vector.tensor_copy(xs[:], xs_tab[:].indirect(offs_t[:]))
+
+        nl = keep.tile([P, V], F32, name="nl", align_bytes=64)
+        nc.vector.tensor_copy(nl[:], nl_tab[:].indirect(anc_t[:]))
+        w_bf = keep.tile([P, PACK, P, PACK], BF16, name="w_bf", align_bytes=64)
+        half = P // 2
+        nc.scalar.copy(
+            out=w_bf[:, :, 0:half, :].rearrange("p t m j -> p m j t"),
+            in_=w_raw[0][:].rearrange("p j (m t) -> p m j t", t=PACK),
+        )
+        nc.scalar.copy(
+            out=w_bf[:, :, half:P, :].rearrange("p t m j -> p m j t"),
+            in_=w_raw[1][:].rearrange("p j (m t) -> p m j t", t=PACK),
+        )
+        nl_ps = once.tile([P, V // P, P], F32, name="nl_ps")
+        for b in range(V // P):
+            nc.tensor.transpose(nl_ps[:, b, :], nl[:, b * P : (b + 1) * P], ident[:])
+        nl_col = keep.tile([P, V // P, 2], F32, name="nl_col")
+        nc.scalar.copy(out=nl_col[:], in_=nl_ps[:, :, 0:2])
+        nn_ps = once.tile([P, V], F32, name="nn_ps")
+        loc_ps = once.tile([P, V], F32, name="loc_ps")
+        for b in range(V // P):
+            nc.tensor.transpose(nn_ps[:, b * P : (b + 1) * P], nl_col[:, b, 0:1].to_broadcast([P, P]), ident[:])
+        for b in range(V // P):
+            nc.tensor.transpose(loc_ps[:, b * P : (b + 1) * P], nl_col[:, b, 1:2].to_broadcast([P, P]), ident[:])
+        nn_row = keep.tile([P, V], F32, name="nn_row")
+        nc.scalar.copy(out=nn_row[:], in_=nn_ps[:])
+
+        wq = keep.tile([P, H], U32, name="wq", tag="nl_then_w", align_bytes=64)
+        ws = keep.tile([P, H], U8, name="ws", align_bytes=64)
+        nc.vector.quantize_mx(
+            out=wq[:].bitcast(FP8X4), scales=ws[:], in_=w_bf[:].rearrange("p t m j -> p (t m j)")
+        )
+
+        xw = keep.tile([P, S], U32, name="xw", align_bytes=64)
+        h_bf = []
+        for i in range(TILES):
+            cols = slice(i * P, (i + 1) * P)
+            nc.vector.tensor_copy(xw[:, cols], xw_tab[:].indirect(offs_t[:, i * 8 : (i + 1) * 8]))
+            h_ps = h_banks.tile([P, PACK, P], F32, name="h_ps")
+            for j in range(PACK):
+                wc = slice(j * P, (j + 1) * P)
+                nc.tensor.matmul_mx(
+                    out=h_ps[:, j, :],
+                    lhsT=wq[:, wc].bitcast(FP8X4),
+                    lhsT_scale=ws[:, wc],
+                    rhs=xw[:, cols].bitcast(FP8X4),
+                    rhs_scale=xs[:, cols],
+                    start=True,
+                    stop=True,
+                )
+            hb = ring.tile([P, P, PACK], BF16, name="hb", align_bytes=64)
+            nc.scalar.copy(out=hb[:], in_=h_ps[:].rearrange("p j t -> p t j"))
+            h_bf.append(hb)
+
+        ew = keep.tile([P, V], U32, name="ew", align_bytes=64)
+        es = keep.tile([P, V], U8, name="es", align_bytes=64)
+        nc.vector.tensor_copy(es[:], es_tab[:].indirect(anc_t[:]))
+        nc.vector.tensor_copy(ew[:], ew_tab[:].indirect(anc_t[:]))
+        hq_all = keep.tile([P, S], U32, name="hq_all", tag="e_then_h", align_bytes=64)
+
+        y_list = []
+        for i in range(TILES):
+            hq = hq_all[:, i * P : (i + 1) * P]
+            hs = ring.tile([P, P], U8, name="hs", align_bytes=64)
+            nc.vector.quantize_mx(
+                out=hq.bitcast(FP8X4), scales=hs[:], in_=h_bf[i][:].rearrange("p t j -> p (t j)")
+            )
+            y_list.append((hq, hs))
+
+        for i in range(TILES):
+            hq, hs = y_list[i]
+            y_ps = y_banks.tile([P, V], F32, name="y_ps")
+            nc.tensor.matmul_mx(
+                out=y_ps[:],
+                lhsT=hq.bitcast(FP8X4),
+                lhsT_scale=hs[:],
+                rhs=ew[:].bitcast(FP8X4),
+                rhs_scale=es[:],
+                start=True,
+                stop=True,
+            )
+            part = ring.tile([P, V], F32, name="part")
+            nc.vector.scalar_tensor_tensor(part[:], y_ps[:], 0.6, nn_row[:], ALU.mult, ALU.subtract)
+            arg = ring.tile([P, V], F32, name="arg")
+            nc.vector.scalar_tensor_tensor(arg[:], part[:], own_t[:, i : i + 1], loc_ps[:], ALU.subtract, ALU.mult)
+            aff = ring.tile([P, V], F32, name="aff")
+            total = ring.tile([P, 1], F32, name="total")
+            nc.scalar.activation(aff[:], arg[:], ACT.Exp, scale=iloc_t[:, i : i + 1], accum_out=total[:])
+            deg = ring.tile([P, 1], F32, name="deg")
+            nc.vector.tensor_scalar(deg[:], total[:], 0.01, 0.005, ALU.mult, ALU.add)
+            inv = ring.tile([P, 1], F32, name="inv")
+            nc.vector.reciprocal(inv[:], deg[:])
+            res = ring.tile([P, V], F32, name="res")
+            if i < TILES - 1:
+                nc.scalar.activation(res[:], aff[:], ACT.Copy, scale=inv[:])
+            else:
+                nc.vector.tensor_scalar(res[:], aff[:], inv[:], None, ALU.mult)
+            nc.sync.dma_start(out=out[i * P : (i + 1) * P, :], in_=res[:])

@@ -32,18 +32,18 @@ def tile_picked_ylocsc_norm_p_kernel(
     with ExitStack() as ctx:
         keep = ctx.enter_context(tc.tile_pool(name="keep", bufs=1))
         ring = ctx.enter_context(tc.tile_pool(name="ring", bufs=4))
-        once = ctx.enter_context(tc.psum_pool(name="once", bufs=1))
-        h_banks = ctx.enter_context(tc.psum_pool(name="h_banks", bufs=2))
-        y_banks = ctx.enter_context(tc.psum_pool(name="y_banks", bufs=3))
+        loc_bank = ctx.enter_context(tc.psum_pool(name="loc_bank", bufs=1))
+        h_banks = ctx.enter_context(tc.psum_pool(name="h_banks", bufs=3))
+        y_banks = ctx.enter_context(tc.psum_pool(name="y_banks", bufs=4))
 
         offs_t = keep.tile([P, S // 16], U16, name="offs_t")
         anc_t = keep.tile([P, V // 16], U16, name="anc_t")
         xw_tab = keep.tile([P, T], U32, name="xw_tab", align_bytes=64)
         xs_tab = keep.tile([P, T], U8, name="xs_tab", align_bytes=64)
-        ew_tab = keep.tile([P, W], U32, name="ew_tab", tag="e_then_h", align_bytes=64)
-        es_tab = keep.tile([P, W], U8, name="es_tab", align_bytes=64)
-        nl_tab = keep.tile([P, W], F32, name="nl_tab", tag="nl_then_w", align_bytes=64)
-        w_raw = [keep.tile([P, PACK, H // 2], F32, name="w_raw%d" % u, align_bytes=64) for u in range(2)]
+        ew_tab = keep.tile([P, W], U32, name="ew_tab", tag="ew_then_h", align_bytes=64)
+        es_tab = keep.tile([P, W], U8, name="es_tab", tag="es_then_h", align_bytes=64)
+        nl_tab = keep.tile([P, W], F32, name="nl_tab", align_bytes=64)
+        w_raw = [keep.tile([P, PACK, H // 2], F32, name="w_raw%d" % u, tag="w_raw%d" % u, align_bytes=64) for u in range(2)]
         own_t = keep.tile([P, TILES], F32, name="own_t")
         iloc_t = keep.tile([P, TILES], F32, name="iloc_t")
         warm = keep.tile([P, 1], F32, name="warm")
@@ -52,54 +52,55 @@ def tile_picked_ylocsc_norm_p_kernel(
 
         nc.vector.memset(xs_tab[:].bitcast(I32), 0)
         nc.vector.memset(warm[:], 0.0)
-        nc.vector.memset(nl_tab[:], 0.0)
         nc.vector.memset(es_tab[:].bitcast(I32), 0)
+        nc.gpsimd.memset(nl_tab[0 : P - 2, :], 0.0)
         nc.scalar.activation(warm_out[:], warm[:], ACT.Exp)
         make_identity(nc, ident[:])
 
-        def load_scales(table, scales):
-            for q in range(4):
-                nc.sync.dma_start(
-                    out=table[32 * q : 32 * q + 4, :].bitcast(I32), in_=scales[0, 4 * q : 4 * q + 4, :].bitcast(I32)
-                )
+        def load_scale_rows(table, scales, q):
+            nc.sync.dma_start(
+                out=table[32 * q : 32 * q + 4, :].bitcast(I32), in_=scales[0, 4 * q : 4 * q + 4, :].bitcast(I32)
+            )
 
         w_rows = w1.rearrange("(p j) c -> p j c", j=PACK)
-        nc.sync.dma_start(out=w_raw[0][:], in_=w_rows[:, :, 0 : H // 2])
-        nc.sync.dma_start(offs_t[:], offs)
-        load_scales(xs_tab, x_scales)
         nc.sync.dma_start(anc_t[:], anc)
+        nc.sync.dma_start(out=nl_tab[P - 2 : P - 1, :], in_=nn[0:1, :])
+        nc.sync.dma_start(out=nl_tab[P - 1 : P, :], in_=loc[0:1, :])
+        nc.sync.dma_start(offs_t[:], offs)
+        for q in range(3):
+            load_scale_rows(xs_tab, x_scales, q)
+        nc.sync.dma_start(out=w_raw[0][:], in_=w_rows[:, :, 0 : H // 2])
+        load_scale_rows(xs_tab, x_scales, 3)
         nc.sync.dma_start(out=w_raw[1][:], in_=w_rows[:, :, H // 2 : H])
-        nc.sync.dma_start(out=nl_tab[0:1, :], in_=nn[0:1, :])
-        nc.sync.dma_start(out=nl_tab[1:2, :], in_=loc[0:1, :])
         nc.sync.dma_start(out=xw_tab[:].bitcast(I32), in_=x_words[0].rearrange("p n t -> p (n t)").bitcast(I32))
-        load_scales(es_tab, e_scales)
+        for q in range(4):
+            load_scale_rows(es_tab, e_scales, q)
         nc.sync.dma_start(out=ew_tab[:].bitcast(I32), in_=e_words[0].rearrange("p n t -> p (n t)").bitcast(I32))
         with nc.allow_non_contiguous_dma(reason="one value a partition"):
             nc.sync.dma_start(out=own_t[:], in_=own.rearrange("(i p) o -> p (i o)", p=P))
             nc.sync.dma_start(out=iloc_t[:], in_=iloc.rearrange("(i p) o -> p (i o)", p=P))
 
-        xs = keep.tile([P, S], U8, name="xs", align_bytes=64)
-        nc.vector.tensor_copy(xs[:], xs_tab[:].indirect(offs_t[:]))
-
         nl = keep.tile([P, V], F32, name="nl", align_bytes=64)
         nc.vector.tensor_copy(nl[:], nl_tab[:].indirect(anc_t[:]))
+        xs = keep.tile([P, S], U8, name="xs", align_bytes=64)
+        nc.vector.tensor_copy(xs[:], xs_tab[:].indirect(offs_t[:]))
         w_bf = keep.tile([P, PACK, P, PACK], BF16, name="w_bf", align_bytes=64)
         half = P // 2
         nc.scalar.copy(
             out=w_bf[:, :, 0:half, :].rearrange("p t m j -> p m j t"),
             in_=w_raw[0][:].rearrange("p j (m t) -> p m j t", t=PACK),
         )
-        nc.scalar.copy(
+        nc.vector.tensor_copy(
             out=w_bf[:, :, half:P, :].rearrange("p t m j -> p m j t"),
             in_=w_raw[1][:].rearrange("p j (m t) -> p m j t", t=PACK),
         )
-        nl_ps = once.tile([P, V // P, P], F32, name="nl_ps")
+        nl_ps = h_banks.tile([P, V // P, P], F32, name="nl_ps", tag="h")
         for b in range(V // P):
             nc.tensor.transpose(nl_ps[:, b, :], nl[:, b * P : (b + 1) * P], ident[:])
-        nl_col = keep.tile([P, V // P, 2], F32, name="nl_col")
-        nc.scalar.copy(out=nl_col[:], in_=nl_ps[:, :, 0:2])
-        nn_ps = once.tile([P, V], F32, name="nn_ps")
-        loc_ps = once.tile([P, V], F32, name="loc_ps")
+        nl_col = keep.tile([P, V // P, 2], F32, name="nl_col", tag="w_raw0", align_bytes=64)
+        nc.scalar.copy(out=nl_col[:], in_=nl_ps[:, :, P - 2 : P])
+        nn_ps = y_banks.tile([P, V], F32, name="nn_ps", tag="y")
+        loc_ps = loc_bank.tile([P, V], F32, name="loc_ps")
         for b in range(V // P):
             nc.tensor.transpose(nn_ps[:, b * P : (b + 1) * P], nl_col[:, b, 0:1].to_broadcast([P, P]), ident[:])
         for b in range(V // P):
@@ -107,7 +108,7 @@ def tile_picked_ylocsc_norm_p_kernel(
         nn_row = keep.tile([P, V], F32, name="nn_row")
         nc.scalar.copy(out=nn_row[:], in_=nn_ps[:])
 
-        wq = keep.tile([P, H], U32, name="wq", tag="nl_then_w", align_bytes=64)
+        wq = keep.tile([P, H], U32, name="wq", align_bytes=64)
         ws = keep.tile([P, H], U8, name="ws", align_bytes=64)
         nc.vector.quantize_mx(
             out=wq[:].bitcast(FP8X4), scales=ws[:], in_=w_bf[:].rearrange("p t m j -> p (t m j)")
@@ -115,66 +116,94 @@ def tile_picked_ylocsc_norm_p_kernel(
 
         xw = keep.tile([P, S], U32, name="xw", align_bytes=64)
         h_bf = []
-        for i in range(TILES):
-            cols = slice(i * P, (i + 1) * P)
-            nc.vector.tensor_copy(xw[:, cols], xw_tab[:].indirect(offs_t[:, i * 8 : (i + 1) * 8]))
-            h_ps = h_banks.tile([P, PACK, P], F32, name="h_ps")
-            for j in range(PACK):
-                wc = slice(j * P, (j + 1) * P)
-                nc.tensor.matmul_mx(
-                    out=h_ps[:, j, :],
-                    lhsT=wq[:, wc].bitcast(FP8X4),
-                    lhsT_scale=ws[:, wc],
-                    rhs=xw[:, cols].bitcast(FP8X4),
-                    rhs_scale=xs[:, cols],
-                    start=True,
-                    stop=True,
-                )
-            hb = ring.tile([P, P, PACK], BF16, name="hb", align_bytes=64)
-            nc.scalar.copy(out=hb[:], in_=h_ps[:].rearrange("p j t -> p t j"))
+        for pair in range(TILES // 2):
+            nc.vector.tensor_copy(
+                xw[:, 2 * P * pair : 2 * P * (pair + 1)], xw_tab[:].indirect(offs_t[:, 16 * pair : 16 * (pair + 1)])
+            )
+            hb = ring.tile([P, 2, P, PACK], BF16, name="hb", align_bytes=64)
+            for u in range(2):
+                cols = slice((2 * pair + u) * P, (2 * pair + u + 1) * P)
+                h_ps = h_banks.tile([P, PACK, P], F32, name="h_ps", tag="h")
+                for j in range(PACK):
+                    wc = slice(j * P, (j + 1) * P)
+                    nc.tensor.matmul_mx(
+                        out=h_ps[:, j, :],
+                        lhsT=wq[:, wc].bitcast(FP8X4),
+                        lhsT_scale=ws[:, wc],
+                        rhs=xw[:, cols].bitcast(FP8X4),
+                        rhs_scale=xs[:, cols],
+                        start=True,
+                        stop=True,
+                    )
+                nc.scalar.copy(out=hb[:, u, :, :], in_=h_ps[:].rearrange("p j t -> p t j"))
             h_bf.append(hb)
 
-        ew = keep.tile([P, V], U32, name="ew", align_bytes=64)
+        halves = [slice(0, V // 2), slice(V // 2, V)]
+        whole = [slice(0, V)]
         es = keep.tile([P, V], U8, name="es", align_bytes=64)
         nc.vector.tensor_copy(es[:], es_tab[:].indirect(anc_t[:]))
-        nc.vector.tensor_copy(ew[:], ew_tab[:].indirect(anc_t[:]))
-        hq_all = keep.tile([P, S], U32, name="hq_all", tag="e_then_h", align_bytes=64)
+        hq_list = []
 
-        y_list = []
-        for i in range(TILES):
-            hq = hq_all[:, i * P : (i + 1) * P]
-            hs = ring.tile([P, P], U8, name="hs", align_bytes=64)
+        def quantize_h(pair, tag):
+            hq = keep.tile([P, 2 * P], U32, name="hq%d" % pair, tag=tag, align_bytes=64)
+            hs = keep.tile([P, 2 * P], U8, name="hs%d" % pair, align_bytes=64)
             nc.vector.quantize_mx(
-                out=hq.bitcast(FP8X4), scales=hs[:], in_=h_bf[i][:].rearrange("p t j -> p (t j)")
+                out=hq[:].bitcast(FP8X4), scales=hs[:], in_=h_bf[pair][:].rearrange("p u t j -> p (u t j)")
             )
-            y_list.append((hq, hs))
+            for u in range(2):
+                hq_list.append((hq[:, u * P : (u + 1) * P], hs[:, u * P : (u + 1) * P]))
 
-        for i in range(TILES):
-            hq, hs = y_list[i]
-            y_ps = y_banks.tile([P, V], F32, name="y_ps")
+        quantize_h(0, "es_then_h")
+        ew = keep.tile([P, V], U32, name="ew", align_bytes=64)
+        for u in range(2):
+            nc.vector.tensor_copy(ew[:, halves[u]], ew_tab[:].indirect(anc_t[:, 16 * u : 16 * (u + 1)]))
+        quantize_h(1, "ew_then_h")
+
+        part = [keep.tile([P, V], F32, name="part%d" % i) for i in range(TILES)]
+        arg = [keep.tile([P, V], F32, name="arg%d" % i) for i in range(TILES)]
+        aff = [keep.tile([P, V], F32, name="aff%d" % i) for i in range(TILES)]
+        res = [keep.tile([P, V], F32, name="res%d" % i) for i in range(TILES)]
+
+        def product(i, c):
+            hq, hs = hq_list[i]
+            y_ps = y_banks.tile([P, c.stop - c.start], F32, name="y_ps", tag="y")
             nc.tensor.matmul_mx(
                 out=y_ps[:],
                 lhsT=hq.bitcast(FP8X4),
-                lhsT_scale=hs[:],
-                rhs=ew[:].bitcast(FP8X4),
-                rhs_scale=es[:],
+                lhsT_scale=hs,
+                rhs=ew[:, c].bitcast(FP8X4),
+                rhs_scale=es[:, c],
                 start=True,
                 stop=True,
             )
-            part = ring.tile([P, V], F32, name="part")
-            nc.vector.scalar_tensor_tensor(part[:], y_ps[:], 0.6, nn_row[:], ALU.mult, ALU.subtract)
-            arg = ring.tile([P, V], F32, name="arg")
-            nc.vector.scalar_tensor_tensor(arg[:], part[:], own_t[:, i : i + 1], loc_ps[:], ALU.subtract, ALU.mult)
-            aff = ring.tile([P, V], F32, name="aff")
-            total = ring.tile([P, 1], F32, name="total")
-            nc.scalar.activation(aff[:], arg[:], ACT.Exp, scale=iloc_t[:, i : i + 1], accum_out=total[:])
-            deg = ring.tile([P, 1], F32, name="deg")
-            nc.vector.tensor_scalar(deg[:], total[:], 0.01, 0.005, ALU.mult, ALU.add)
+            nc.vector.scalar_tensor_tensor(part[i][:, c], y_ps[:], 0.6, nn_row[:, c], ALU.mult, ALU.subtract)
+
+        def affinity(i, c, so_far):
+            nc.vector.scalar_tensor_tensor(
+                arg[i][:, c], part[i][:, c], own_t[:, i : i + 1], loc_ps[:, c], ALU.subtract, ALU.mult
+            )
+            total = ring.tile([P, 1], F32, name="total", bufs=5)
+            nc.scalar.activation(aff[i][:, c], arg[i][:, c], ACT.Exp, scale=iloc_t[:, i : i + 1], accum_out=total[:])
+            deg = ring.tile([P, 1], F32, name="deg", bufs=5)
+            if so_far is None:
+                nc.scalar.activation(deg[:], total[:], ACT.Copy, bias=0.5)
+            else:
+                nc.scalar.activation(deg[:], total[:], ACT.Identity, bias=so_far[:])
+            return deg
+
+        def normalise(i, deg, engine, spans):
             inv = ring.tile([P, 1], F32, name="inv")
             nc.vector.reciprocal(inv[:], deg[:])
-            res = ring.tile([P, V], F32, name="res")
-            if i < TILES - 1:
-                nc.scalar.activation(res[:], aff[:], ACT.Copy, scale=inv[:])
-            else:
-                nc.vector.tensor_scalar(res[:], aff[:], inv[:], None, ALU.mult)
-            nc.sync.dma_start(out=out[i * P : (i + 1) * P, :], in_=res[:])
+            for c in spans:
+                engine.tensor_scalar(res[i][:, c], aff[i][:, c], inv[:], 100.0, ALU.mult, ALU.mult)
+                nc.sync.dma_start(out=out[i * P : (i + 1) * P, c], in_=res[i][:, c])
+
+        last = TILES - 1
+        for c in halves:
+            product(0, c)
+        for i in range(last):
+            product(i + 1, whole[0] if i + 1 < last else halves[0])
+            normalise(i, affinity(i, whole[0], None), nc.gpsimd, whole)
+        product(last, halves[1])
+        deg = affinity(last, halves[0], None)
+        normalise(last, affinity(last, halves[1], deg), nc.vector, halves)

@@ -15,6 +15,8 @@ ACT = mybir.ActivationFunctionType
 
 P = 128
 PACK = 4
+QUADRANT = 32
+LANES = 16
 K = 512
 H = 512
 S = 512
@@ -31,52 +33,50 @@ def tile_picked_ylocsc_norm_p_kernel(
     nc = tc.nc
     with ExitStack() as ctx:
         keep = ctx.enter_context(tc.tile_pool(name="keep", bufs=1))
-        ring = ctx.enter_context(tc.tile_pool(name="ring", bufs=4))
+        ring = ctx.enter_context(tc.tile_pool(name="ring", bufs=TILES))
         loc_bank = ctx.enter_context(tc.psum_pool(name="loc_bank", bufs=1))
         h_banks = ctx.enter_context(tc.psum_pool(name="h_banks", bufs=3))
         y_banks = ctx.enter_context(tc.psum_pool(name="y_banks", bufs=4))
 
-        offs_t = keep.tile([P, S // 16], U16, name="offs_t")
-        anc_t = keep.tile([P, V // 16], U16, name="anc_t")
+        offs_t = keep.tile([P, S // LANES], U16, name="offs_t")
+        anc_t = keep.tile([P, V // LANES], U16, name="anc_t")
         xw_tab = keep.tile([P, T], U32, name="xw_tab", align_bytes=64)
         xs_tab = keep.tile([P, T], U8, name="xs_tab", align_bytes=64)
         ew_tab = keep.tile([P, W], U32, name="ew_tab", tag="ew_then_h", align_bytes=64)
         es_tab = keep.tile([P, W], U8, name="es_tab", tag="es_then_h", align_bytes=64)
         nl_tab = keep.tile([P, W], F32, name="nl_tab", align_bytes=64)
-        w_raw = [keep.tile([P, PACK, H // 2], F32, name="w_raw%d" % u, tag="w_raw%d" % u, align_bytes=64) for u in range(2)]
+        w_raw = [
+            keep.tile([P, PACK, H // 2], F32, name="w_raw%d" % u, tag="w_raw%d" % u, align_bytes=64) for u in range(2)
+        ]
         own_t = keep.tile([P, TILES], F32, name="own_t")
         iloc_t = keep.tile([P, TILES], F32, name="iloc_t")
-        warm = keep.tile([P, 1], F32, name="warm")
-        warm_out = keep.tile([P, 1], F32, name="warm_out")
         ident = keep.tile([P, P], F32, name="ident")
 
+        nn_part, loc_part = P - 2, P - 1
         nc.vector.memset(xs_tab[:].bitcast(I32), 0)
-        nc.vector.memset(warm[:], 0.0)
-        nc.vector.memset(es_tab[:].bitcast(I32), 0)
-        nc.gpsimd.memset(nl_tab[0 : P - 2, :], 0.0)
-        nc.scalar.activation(warm_out[:], warm[:], ACT.Exp)
+        nc.vector.memset(nl_tab[0:nn_part, :], 0.0)
+        nc.gpsimd.memset(es_tab[:].bitcast(I32), 0)
         make_identity(nc, ident[:])
 
-        def load_scale_rows(table, scales, q):
-            nc.sync.dma_start(
-                out=table[32 * q : 32 * q + 4, :].bitcast(I32), in_=scales[0, 4 * q : 4 * q + 4, :].bitcast(I32)
-            )
+        def load_scales(table, scales):
+            for r in range(PACK):
+                nc.sync.dma_start(out=table[r:P:QUADRANT, :].bitcast(I32), in_=scales[0, r:16:PACK, :].bitcast(I32))
+
+        def load_words(table, words):
+            nc.sync.dma_start(out=table[:].bitcast(I32), in_=words[0].rearrange("p n t -> p (n t)").bitcast(I32))
 
         w_rows = w1.rearrange("(p j) c -> p j c", j=PACK)
         nc.sync.dma_start(anc_t[:], anc)
-        nc.sync.dma_start(out=nl_tab[P - 2 : P - 1, :], in_=nn[0:1, :])
-        nc.sync.dma_start(out=nl_tab[P - 1 : P, :], in_=loc[0:1, :])
-        nc.sync.dma_start(offs_t[:], offs)
-        for q in range(3):
-            load_scale_rows(xs_tab, x_scales, q)
+        nc.sync.dma_start(out=nl_tab[nn_part : nn_part + 1, :], in_=nn[0:1, :])
+        nc.sync.dma_start(out=nl_tab[loc_part : loc_part + 1, :], in_=loc[0:1, :])
         nc.sync.dma_start(out=w_raw[0][:], in_=w_rows[:, :, 0 : H // 2])
-        load_scale_rows(xs_tab, x_scales, 3)
+        nc.sync.dma_start(offs_t[:], offs)
+        load_scales(xs_tab, x_scales)
         nc.sync.dma_start(out=w_raw[1][:], in_=w_rows[:, :, H // 2 : H])
-        nc.sync.dma_start(out=xw_tab[:].bitcast(I32), in_=x_words[0].rearrange("p n t -> p (n t)").bitcast(I32))
-        for q in range(4):
-            load_scale_rows(es_tab, e_scales, q)
-        nc.sync.dma_start(out=ew_tab[:].bitcast(I32), in_=e_words[0].rearrange("p n t -> p (n t)").bitcast(I32))
-        with nc.allow_non_contiguous_dma(reason="one value a partition"):
+        load_words(xw_tab, x_words)
+        load_scales(es_tab, e_scales)
+        load_words(ew_tab, e_words)
+        with nc.allow_non_contiguous_dma(reason="point 128 i + p goes to partition p, column i"):
             nc.sync.dma_start(out=own_t[:], in_=own.rearrange("(i p) o -> p (i o)", p=P))
             nc.sync.dma_start(out=iloc_t[:], in_=iloc.rearrange("(i p) o -> p (i o)", p=P))
 
@@ -84,88 +84,95 @@ def tile_picked_ylocsc_norm_p_kernel(
         nc.vector.tensor_copy(nl[:], nl_tab[:].indirect(anc_t[:]))
         xs = keep.tile([P, S], U8, name="xs", align_bytes=64)
         nc.vector.tensor_copy(xs[:], xs_tab[:].indirect(offs_t[:]))
+
         w_bf = keep.tile([P, PACK, P, PACK], BF16, name="w_bf", align_bytes=64)
-        half = P // 2
-        nc.scalar.copy(
-            out=w_bf[:, :, 0:half, :].rearrange("p t m j -> p m j t"),
-            in_=w_raw[0][:].rearrange("p j (m t) -> p m j t", t=PACK),
-        )
-        nc.vector.tensor_copy(
-            out=w_bf[:, :, half:P, :].rearrange("p t m j -> p m j t"),
-            in_=w_raw[1][:].rearrange("p j (m t) -> p m j t", t=PACK),
-        )
+        quarter = P // 4
+
+        def round_w(copy, first, count):
+            u, m0 = divmod(first, P // 2)
+            copy(
+                out=w_bf[:, :, first : first + count, :].rearrange("p t m j -> p m j t"),
+                in_=w_raw[u][:, :, PACK * m0 : PACK * (m0 + count)].rearrange("p j (m t) -> p m j t", t=PACK),
+            )
+
+        round_w(nc.scalar.copy, 0, 2 * quarter)
+        round_w(nc.scalar.copy, 2 * quarter, quarter)
+        round_w(nc.vector.tensor_copy, 3 * quarter, quarter)
+
         nl_ps = h_banks.tile([P, V // P, P], F32, name="nl_ps", tag="h")
         for b in range(V // P):
             nc.tensor.transpose(nl_ps[:, b, :], nl[:, b * P : (b + 1) * P], ident[:])
-        nl_col = keep.tile([P, V // P, 2], F32, name="nl_col", tag="w_raw0", align_bytes=64)
-        nc.scalar.copy(out=nl_col[:], in_=nl_ps[:, :, P - 2 : P])
+        nl_col = keep.tile([P, V // P, 2], F32, name="nl_col", tag="w_raw1", align_bytes=64)
+        nc.scalar.copy(out=nl_col[:], in_=nl_ps[:, :, nn_part:P])
         nn_ps = y_banks.tile([P, V], F32, name="nn_ps", tag="y")
         loc_ps = loc_bank.tile([P, V], F32, name="loc_ps")
-        for b in range(V // P):
-            nc.tensor.transpose(nn_ps[:, b * P : (b + 1) * P], nl_col[:, b, 0:1].to_broadcast([P, P]), ident[:])
-        for b in range(V // P):
-            nc.tensor.transpose(loc_ps[:, b * P : (b + 1) * P], nl_col[:, b, 1:2].to_broadcast([P, P]), ident[:])
+        for row, bank in enumerate((nn_ps, loc_ps)):
+            for b in range(V // P):
+                column = nl_col[:, b, row : row + 1].to_broadcast([P, P])
+                nc.tensor.transpose(bank[:, b * P : (b + 1) * P], column, ident[:])
         nn_row = keep.tile([P, V], F32, name="nn_row")
         nc.scalar.copy(out=nn_row[:], in_=nn_ps[:])
 
         wq = keep.tile([P, H], U32, name="wq", align_bytes=64)
         ws = keep.tile([P, H], U8, name="ws", align_bytes=64)
-        nc.vector.quantize_mx(
-            out=wq[:].bitcast(FP8X4), scales=ws[:], in_=w_bf[:].rearrange("p t m j -> p (t m j)")
-        )
+        nc.vector.quantize_mx(out=wq[:].bitcast(FP8X4), scales=ws[:], in_=w_bf[:].rearrange("p t m j -> p (t m j)"))
 
         xw = keep.tile([P, S], U32, name="xw", align_bytes=64)
+        per_tile = P // LANES
         h_bf = []
         for pair in range(TILES // 2):
-            nc.vector.tensor_copy(
-                xw[:, 2 * P * pair : 2 * P * (pair + 1)], xw_tab[:].indirect(offs_t[:, 16 * pair : 16 * (pair + 1)])
-            )
-            hb = ring.tile([P, 2, P, PACK], BF16, name="hb", align_bytes=64)
+            for a, b in [(0, 1), (1, 2)] if pair == 0 else [(2, 4)]:
+                nc.vector.tensor_copy(
+                    xw[:, P * a : P * b], xw_tab[:].indirect(offs_t[:, per_tile * a : per_tile * b])
+                )
+            h_pair = ring.tile([P, 2, P, PACK], BF16, name="h_pair", align_bytes=64)
             for u in range(2):
-                cols = slice((2 * pair + u) * P, (2 * pair + u + 1) * P)
+                points = slice((2 * pair + u) * P, (2 * pair + u + 1) * P)
                 h_ps = h_banks.tile([P, PACK, P], F32, name="h_ps", tag="h")
-                for j in range(PACK):
-                    wc = slice(j * P, (j + 1) * P)
+                for t in range(PACK):
+                    block = slice(t * P, (t + 1) * P)
                     nc.tensor.matmul_mx(
-                        out=h_ps[:, j, :],
-                        lhsT=wq[:, wc].bitcast(FP8X4),
-                        lhsT_scale=ws[:, wc],
-                        rhs=xw[:, cols].bitcast(FP8X4),
-                        rhs_scale=xs[:, cols],
+                        out=h_ps[:, t, :],
+                        lhsT=wq[:, block].bitcast(FP8X4),
+                        lhsT_scale=ws[:, block],
+                        rhs=xw[:, points].bitcast(FP8X4),
+                        rhs_scale=xs[:, points],
                         start=True,
                         stop=True,
                     )
-                nc.scalar.copy(out=hb[:, u, :, :], in_=h_ps[:].rearrange("p j t -> p t j"))
-            h_bf.append(hb)
+                nc.scalar.copy(out=h_pair[:, u, :, :], in_=h_ps[:].rearrange("p t n -> p n t"))
+            h_bf.append(h_pair)
 
         halves = [slice(0, V // 2), slice(V // 2, V)]
-        whole = [slice(0, V)]
-        es = keep.tile([P, V], U8, name="es", align_bytes=64)
-        nc.vector.tensor_copy(es[:], es_tab[:].indirect(anc_t[:]))
-        hq_list = []
+        whole = slice(0, V)
+        h_mx = []
 
         def quantize_h(pair, tag):
             hq = keep.tile([P, 2 * P], U32, name="hq%d" % pair, tag=tag, align_bytes=64)
             hs = keep.tile([P, 2 * P], U8, name="hs%d" % pair, align_bytes=64)
             nc.vector.quantize_mx(
-                out=hq[:].bitcast(FP8X4), scales=hs[:], in_=h_bf[pair][:].rearrange("p u t j -> p (u t j)")
+                out=hq[:].bitcast(FP8X4), scales=hs[:], in_=h_bf[pair][:].rearrange("p u n t -> p (u n t)")
             )
             for u in range(2):
-                hq_list.append((hq[:, u * P : (u + 1) * P], hs[:, u * P : (u + 1) * P]))
+                h_mx.append((hq[:, u * P : (u + 1) * P], hs[:, u * P : (u + 1) * P]))
 
+        es = keep.tile([P, V], U8, name="es", align_bytes=64)
+        nc.vector.tensor_copy(es[:], es_tab[:].indirect(anc_t[:]))
         quantize_h(0, "es_then_h")
         ew = keep.tile([P, V], U32, name="ew", align_bytes=64)
-        for u in range(2):
-            nc.vector.tensor_copy(ew[:, halves[u]], ew_tab[:].indirect(anc_t[:, 16 * u : 16 * (u + 1)]))
+        for c in halves:
+            nc.vector.tensor_copy(ew[:, c], ew_tab[:].indirect(anc_t[:, c.start // LANES : c.stop // LANES]))
         quantize_h(1, "ew_then_h")
 
-        part = [keep.tile([P, V], F32, name="part%d" % i) for i in range(TILES)]
+        part = {}
         arg = [keep.tile([P, V], F32, name="arg%d" % i) for i in range(TILES)]
         aff = [keep.tile([P, V], F32, name="aff%d" % i) for i in range(TILES)]
         res = [keep.tile([P, V], F32, name="res%d" % i) for i in range(TILES)]
 
         def product(i, c):
-            hq, hs = hq_list[i]
+            hq, hs = h_mx[i]
+            if i not in part:
+                part[i] = ring.tile([P, V], F32, name="part", bufs=2)
             y_ps = y_banks.tile([P, c.stop - c.start], F32, name="y_ps", tag="y")
             nc.tensor.matmul_mx(
                 out=y_ps[:],
@@ -178,32 +185,45 @@ def tile_picked_ylocsc_norm_p_kernel(
             )
             nc.vector.scalar_tensor_tensor(part[i][:, c], y_ps[:], 0.6, nn_row[:, c], ALU.mult, ALU.subtract)
 
-        def affinity(i, c, so_far):
+        def affinity(i, c):
             nc.vector.scalar_tensor_tensor(
                 arg[i][:, c], part[i][:, c], own_t[:, i : i + 1], loc_ps[:, c], ALU.subtract, ALU.mult
             )
-            total = ring.tile([P, 1], F32, name="total", bufs=5)
+            total = ring.tile([P, 1], F32, name="total", bufs=TILES + 1)
             nc.scalar.activation(aff[i][:, c], arg[i][:, c], ACT.Exp, scale=iloc_t[:, i : i + 1], accum_out=total[:])
-            deg = ring.tile([P, 1], F32, name="deg", bufs=5)
-            if so_far is None:
-                nc.scalar.activation(deg[:], total[:], ACT.Copy, bias=0.5)
-            else:
-                nc.scalar.activation(deg[:], total[:], ACT.Identity, bias=so_far[:])
+            return total
+
+        def hundredth_degree(total):
+            deg = ring.tile([P, 1], F32, name="deg")
+            nc.scalar.activation(deg[:], total[:], ACT.Copy, scale=0.01, bias=0.005)
             return deg
 
-        def normalise(i, deg, engine, spans):
+        def invert(deg):
             inv = ring.tile([P, 1], F32, name="inv")
             nc.vector.reciprocal(inv[:], deg[:])
-            for c in spans:
-                engine.tensor_scalar(res[i][:, c], aff[i][:, c], inv[:], 100.0, ALU.mult, ALU.mult)
-                nc.sync.dma_start(out=out[i * P : (i + 1) * P, c], in_=res[i][:, c])
+            return inv
 
-        last = TILES - 1
+        def store(i, c):
+            nc.sync.dma_start(out=out[i * P : (i + 1) * P, c], in_=res[i][:, c])
+
         for c in halves:
             product(0, c)
-        for i in range(last):
-            product(i + 1, whole[0] if i + 1 < last else halves[0])
-            normalise(i, affinity(i, whole[0], None), nc.gpsimd, whole)
-        product(last, halves[1])
-        deg = affinity(last, halves[0], None)
-        normalise(last, affinity(last, halves[1], deg), nc.vector, halves)
+        product(1, whole)
+        deg0 = hundredth_degree(affinity(0, whole))
+        product(2, whole)
+        deg1 = hundredth_degree(affinity(1, whole))
+        nc.scalar.activation(res[0][:], aff[0][:], ACT.Copy, scale=invert(deg0)[:])
+        store(0, whole)
+        product(3, halves[0])
+        deg2 = hundredth_degree(affinity(2, whole))
+        product(3, halves[1])
+        totals = [affinity(3, c) for c in halves]
+        for i, deg in ((1, deg1), (2, deg2)):
+            nc.vector.tensor_scalar(res[i][:], aff[i][:], invert(deg)[:], None, ALU.mult)
+            store(i, whole)
+        deg3 = ring.tile([P, 1], F32, name="deg")
+        nc.vector.tensor_scalar(deg3[:], totals[0][:], totals[1][:], 0.5, ALU.add, ALU.add)
+        inv3 = invert(deg3)
+        for c in halves:
+            nc.vector.tensor_scalar(res[3][:, c], aff[3][:, c], inv3[:], 100.0, ALU.mult, ALU.mult)
+            store(3, c)

@@ -16,6 +16,7 @@ ACT = mybir.ActivationFunctionType
 P = 128
 PACK = 4
 QUADRANT = 32
+BLOCKS = 16
 LANES = 16
 K = 512
 H = 512
@@ -60,7 +61,7 @@ def tile_picked_ylocsc_norm_p_kernel(
 
         def load_scales(table, scales):
             for r in range(PACK):
-                nc.sync.dma_start(out=table[r:P:QUADRANT, :].bitcast(I32), in_=scales[0, r:16:PACK, :].bitcast(I32))
+                nc.sync.dma_start(out=table[r:P:QUADRANT, :].bitcast(I32), in_=scales[0, r:BLOCKS:PACK, :].bitcast(I32))
 
         def load_words(table, words):
             nc.sync.dma_start(out=table[:].bitcast(I32), in_=words[0].rearrange("p n t -> p (n t)").bitcast(I32))
@@ -86,7 +87,7 @@ def tile_picked_ylocsc_norm_p_kernel(
         nc.vector.tensor_copy(xs[:], xs_tab[:].indirect(offs_t[:]))
 
         w_bf = keep.tile([P, PACK, P, PACK], BF16, name="w_bf", align_bytes=64)
-        quarter = P // 4
+        scalar_share = 88
 
         def round_w(copy, first, count):
             u, m0 = divmod(first, P // 2)
@@ -95,14 +96,14 @@ def tile_picked_ylocsc_norm_p_kernel(
                 in_=w_raw[u][:, :, PACK * m0 : PACK * (m0 + count)].rearrange("p j (m t) -> p m j t", t=PACK),
             )
 
-        round_w(nc.scalar.copy, 0, 2 * quarter)
-        round_w(nc.scalar.copy, 2 * quarter, quarter)
-        round_w(nc.vector.tensor_copy, 3 * quarter, quarter)
+        round_w(nc.scalar.copy, 0, P // 2)
+        round_w(nc.scalar.copy, P // 2, scalar_share - P // 2)
+        round_w(nc.vector.tensor_copy, scalar_share, P - scalar_share)
 
         nl_ps = h_banks.tile([P, V // P, P], F32, name="nl_ps", tag="h")
         for b in range(V // P):
             nc.tensor.transpose(nl_ps[:, b, :], nl[:, b * P : (b + 1) * P], ident[:])
-        nl_col = keep.tile([P, V // P, 2], F32, name="nl_col", tag="w_raw1", align_bytes=64)
+        nl_col = keep.tile([P, V // P, 2], F32, name="nl_col", tag="w_raw0", align_bytes=64)
         nc.scalar.copy(out=nl_col[:], in_=nl_ps[:, :, nn_part:P])
         nn_ps = y_banks.tile([P, V], F32, name="nn_ps", tag="y")
         loc_ps = loc_bank.tile([P, V], F32, name="loc_ps")
@@ -110,7 +111,7 @@ def tile_picked_ylocsc_norm_p_kernel(
             for b in range(V // P):
                 column = nl_col[:, b, row : row + 1].to_broadcast([P, P])
                 nc.tensor.transpose(bank[:, b * P : (b + 1) * P], column, ident[:])
-        nn_row = keep.tile([P, V], F32, name="nn_row")
+        nn_row = keep.tile([P, V], F32, name="nn_row", tag="w_raw1", align_bytes=64)
         nc.scalar.copy(out=nn_row[:], in_=nn_ps[:])
 
         wq = keep.tile([P, H], U32, name="wq", align_bytes=64)
@@ -194,13 +195,13 @@ def tile_picked_ylocsc_norm_p_kernel(
             return total
 
         def hundredth_degree(total):
-            deg = ring.tile([P, 1], F32, name="deg")
-            nc.scalar.activation(deg[:], total[:], ACT.Copy, scale=0.01, bias=0.005)
-            return deg
+            hundredth = ring.tile([P, 1], F32, name="divisor")
+            nc.scalar.activation(hundredth[:], total[:], ACT.Copy, scale=0.01, bias=0.005)
+            return hundredth
 
-        def invert(deg):
+        def invert(divisor):
             inv = ring.tile([P, 1], F32, name="inv")
-            nc.vector.reciprocal(inv[:], deg[:])
+            nc.vector.reciprocal(inv[:], divisor[:])
             return inv
 
         def store(i, c):
@@ -209,20 +210,24 @@ def tile_picked_ylocsc_norm_p_kernel(
         for c in halves:
             product(0, c)
         product(1, whole)
-        deg0 = hundredth_degree(affinity(0, whole))
+        hundredth0 = hundredth_degree(affinity(0, whole))
         product(2, whole)
-        deg1 = hundredth_degree(affinity(1, whole))
-        nc.scalar.activation(res[0][:], aff[0][:], ACT.Copy, scale=invert(deg0)[:])
+        hundredth1 = hundredth_degree(affinity(1, whole))
+        nc.scalar.activation(res[0][:], aff[0][:], ACT.Copy, scale=invert(hundredth0)[:])
         store(0, whole)
         product(3, halves[0])
-        deg2 = hundredth_degree(affinity(2, whole))
+        total2 = affinity(2, whole)
         product(3, halves[1])
-        totals = [affinity(3, c) for c in halves]
-        for i, deg in ((1, deg1), (2, deg2)):
-            nc.vector.tensor_scalar(res[i][:], aff[i][:], invert(deg)[:], None, ALU.mult)
-            store(i, whole)
-        deg3 = ring.tile([P, 1], F32, name="deg")
-        nc.vector.tensor_scalar(deg3[:], totals[0][:], totals[1][:], 0.5, ALU.add, ALU.add)
+        inv1 = invert(hundredth1)
+        totals3 = [affinity(3, c) for c in halves]
+        hundredth2 = ring.tile([P, 1], F32, name="divisor")
+        nc.vector.tensor_scalar(hundredth2[:], total2[:], 0.01, 0.005, ALU.mult, ALU.add)
+        nc.vector.tensor_scalar(res[1][:], aff[1][:], inv1[:], None, ALU.mult)
+        store(1, whole)
+        nc.vector.tensor_scalar(res[2][:], aff[2][:], invert(hundredth2)[:], None, ALU.mult)
+        store(2, whole)
+        deg3 = ring.tile([P, 1], F32, name="divisor")
+        nc.vector.tensor_scalar(deg3[:], totals3[0][:], totals3[1][:], 0.5, ALU.add, ALU.add)
         inv3 = invert(deg3)
         for c in halves:
             nc.vector.tensor_scalar(res[3][:, c], aff[3][:, c], inv3[:], 100.0, ALU.mult, ALU.mult)

from contextlib import ExitStack

import concourse.mybir as mybir
from concourse.masks import make_identity

F32 = mybir.dt.float32
BF16 = mybir.dt.bfloat16
I32 = mybir.dt.int32
U32 = mybir.dt.uint32
U16 = mybir.dt.uint16
U8 = mybir.dt.uint8
FP8X4 = mybir.dt.float8_e4m3fn_x4
ALU = mybir.AluOpType
ACT = mybir.ActivationFunctionType

P = 128
PACK = 4
QUADRANT = 32
BLOCKS = 16
LANES = 16
K = 512
H = 512
S = 512
V = 512
T = 1024
W = 2048
TILES = S // P
FLOPS = 2 * K * H * S + 2 * H * S * V


def tile_picked_ylocsc_norm_p_kernel(
    tc, x_words, x_scales, w1, e_words, e_scales, nn, own, loc, iloc, offs, anc, out
):
    nc = tc.nc
    with ExitStack() as ctx:
        keep = ctx.enter_context(tc.tile_pool(name="keep", bufs=1))
        ring = ctx.enter_context(tc.tile_pool(name="ring", bufs=TILES))
        loc_bank = ctx.enter_context(tc.psum_pool(name="loc_bank", bufs=1))
        h_banks = ctx.enter_context(tc.psum_pool(name="h_banks", bufs=3))
        y_banks = ctx.enter_context(tc.psum_pool(name="y_banks", bufs=4))

        offs_t = keep.tile([P, S // LANES], U16, name="offs_t")
        anc_t = keep.tile([P, V // LANES], U16, name="anc_t")
        xw_tab = keep.tile([P, T], U32, name="xw_tab", align_bytes=64)
        xs_tab = keep.tile([P, T], U8, name="xs_tab", align_bytes=64)
        ew_tab = keep.tile([P, W], U32, name="ew_tab", tag="ew_then_h", align_bytes=64)
        es_tab = keep.tile([P, W], U8, name="es_tab", tag="es_then_h", align_bytes=64)
        nl_tab = keep.tile([P, W], F32, name="nl_tab", align_bytes=64)
        w_raw = [
            keep.tile([P, PACK, H // 2], F32, name="w_raw%d" % u, tag="w_raw%d" % u, align_bytes=64) for u in range(2)
        ]
        own_t = keep.tile([P, TILES], F32, name="own_t")
        iloc_t = keep.tile([P, TILES], F32, name="iloc_t")
        ident = keep.tile([P, P], F32, name="ident")

        nn_part, loc_part = P - 2, P - 1
        nc.vector.memset(xs_tab[:].bitcast(I32), 0)
        nc.vector.memset(nl_tab[0:nn_part, :], 0.0)
        nc.gpsimd.memset(es_tab[:].bitcast(I32), 0)
        make_identity(nc, ident[:])

        def load_scales(table, scales):
            for r in range(PACK):
                nc.sync.dma_start(out=table[r:P:QUADRANT, :].bitcast(I32), in_=scales[0, r:BLOCKS:PACK, :].bitcast(I32))

        def load_words(table, words):
            nc.sync.dma_start(out=table[:].bitcast(I32), in_=words[0].rearrange("p n t -> p (n t)").bitcast(I32))

        w_rows = w1.rearrange("(p j) c -> p j c", j=PACK)
        nc.sync.dma_start(anc_t[:], anc)
        nc.sync.dma_start(out=nl_tab[nn_part : nn_part + 1, :], in_=nn[0:1, :])
        nc.sync.dma_start(out=nl_tab[loc_part : loc_part + 1, :], in_=loc[0:1, :])
        nc.sync.dma_start(out=w_raw[0][:], in_=w_rows[:, :, 0 : H // 2])
        nc.sync.dma_start(offs_t[:], offs)
        load_scales(xs_tab, x_scales)
        nc.sync.dma_start(out=w_raw[1][:], in_=w_rows[:, :, H // 2 : H])
        load_words(xw_tab, x_words)
        load_scales(es_tab, e_scales)
        load_words(ew_tab, e_words)
        with nc.allow_non_contiguous_dma(reason="point 128 i + p goes to partition p, column i"):
            nc.sync.dma_start(out=own_t[:], in_=own.rearrange("(i p) o -> p (i o)", p=P))
            nc.sync.dma_start(out=iloc_t[:], in_=iloc.rearrange("(i p) o -> p (i o)", p=P))

        nl = keep.tile([P, V], F32, name="nl", align_bytes=64)
        nc.vector.tensor_copy(nl[:], nl_tab[:].indirect(anc_t[:]))
        xs = keep.tile([P, S], U8, name="xs", align_bytes=64)
        nc.vector.tensor_copy(xs[:], xs_tab[:].indirect(offs_t[:]))

        w_bf = keep.tile([P, PACK, P, PACK], BF16, name="w_bf", align_bytes=64)
        scalar_share = 88

        def round_w(copy, first, count):
            u, m0 = divmod(first, P // 2)
            copy(
                out=w_bf[:, :, first : first + count, :].rearrange("p t m j -> p m j t"),
                in_=w_raw[u][:, :, PACK * m0 : PACK * (m0 + count)].rearrange("p j (m t) -> p m j t", t=PACK),
            )

        round_w(nc.scalar.copy, 0, P // 2)
        round_w(nc.scalar.copy, P // 2, scalar_share - P // 2)
        round_w(nc.vector.tensor_copy, scalar_share, P - scalar_share)

        nl_ps = h_banks.tile([P, V // P, P], F32, name="nl_ps", tag="h")
        for b in range(V // P):
            nc.tensor.transpose(nl_ps[:, b, :], nl[:, b * P : (b + 1) * P], ident[:])
        nl_col = keep.tile([P, V // P, 2], F32, name="nl_col", tag="w_raw0", align_bytes=64)
        nc.scalar.copy(out=nl_col[:], in_=nl_ps[:, :, nn_part:P])
        nn_ps = y_banks.tile([P, V], F32, name="nn_ps", tag="y")
        loc_ps = loc_bank.tile([P, V], F32, name="loc_ps")
        for row, bank in enumerate((nn_ps, loc_ps)):
            for b in range(V // P):
                column = nl_col[:, b, row : row + 1].to_broadcast([P, P])
                nc.tensor.transpose(bank[:, b * P : (b + 1) * P], column, ident[:])
        nn_row = keep.tile([P, V], F32, name="nn_row", tag="w_raw1", align_bytes=64)
        nc.scalar.copy(out=nn_row[:], in_=nn_ps[:])

        wq = keep.tile([P, H], U32, name="wq", align_bytes=64)
        ws = keep.tile([P, H], U8, name="ws", align_bytes=64)
        nc.vector.quantize_mx(out=wq[:].bitcast(FP8X4), scales=ws[:], in_=w_bf[:].rearrange("p t m j -> p (t m j)"))

        xw = keep.tile([P, S], U32, name="xw", align_bytes=64)
        per_tile = P // LANES
        h_bf = []
        for pair in range(TILES // 2):
            for a, b in [(0, 1), (1, 2)] if pair == 0 else [(2, 4)]:
                nc.vector.tensor_copy(
                    xw[:, P * a : P * b], xw_tab[:].indirect(offs_t[:, per_tile * a : per_tile * b])
                )
            h_pair = ring.tile([P, 2, P, PACK], BF16, name="h_pair", align_bytes=64)
            for u in range(2):
                points = slice((2 * pair + u) * P, (2 * pair + u + 1) * P)
                h_ps = h_banks.tile([P, PACK, P], F32, name="h_ps", tag="h")
                for t in range(PACK):
                    block = slice(t * P, (t + 1) * P)
                    nc.tensor.matmul_mx(
                        out=h_ps[:, t, :],
                        lhsT=wq[:, block].bitcast(FP8X4),
                        lhsT_scale=ws[:, block],
                        rhs=xw[:, points].bitcast(FP8X4),
                        rhs_scale=xs[:, points],
                        start=True,
                        stop=True,
                    )
                nc.scalar.copy(out=h_pair[:, u, :, :], in_=h_ps[:].rearrange("p t n -> p n t"))
            h_bf.append(h_pair)

        halves = [slice(0, V // 2), slice(V // 2, V)]
        whole = slice(0, V)
        h_mx = []

        def quantize_h(pair, tag):
            hq = keep.tile([P, 2 * P], U32, name="hq%d" % pair, tag=tag, align_bytes=64)
            hs = keep.tile([P, 2 * P], U8, name="hs%d" % pair, align_bytes=64)
            nc.vector.quantize_mx(
                out=hq[:].bitcast(FP8X4), scales=hs[:], in_=h_bf[pair][:].rearrange("p u n t -> p (u n t)")
            )
            for u in range(2):
                h_mx.append((hq[:, u * P : (u + 1) * P], hs[:, u * P : (u + 1) * P]))

        es = keep.tile([P, V], U8, name="es", align_bytes=64)
        nc.vector.tensor_copy(es[:], es_tab[:].indirect(anc_t[:]))
        quantize_h(0, "es_then_h")
        ew = keep.tile([P, V], U32, name="ew", align_bytes=64)
        for c in halves:
            nc.vector.tensor_copy(ew[:, c], ew_tab[:].indirect(anc_t[:, c.start // LANES : c.stop // LANES]))
        quantize_h(1, "ew_then_h")

        part = {}
        arg = [keep.tile([P, V], F32, name="arg%d" % i) for i in range(TILES)]
        aff = [keep.tile([P, V], F32, name="aff%d" % i) for i in range(TILES)]
        res = [keep.tile([P, V], F32, name="res%d" % i) for i in range(TILES)]

        def product(i, c):
            hq, hs = h_mx[i]
            if i not in part:
                part[i] = ring.tile([P, V], F32, name="part", bufs=2)
            y_ps = y_banks.tile([P, c.stop - c.start], F32, name="y_ps", tag="y")
            nc.tensor.matmul_mx(
                out=y_ps[:],
                lhsT=hq.bitcast(FP8X4),
                lhsT_scale=hs,
                rhs=ew[:, c].bitcast(FP8X4),
                rhs_scale=es[:, c],
                start=True,
                stop=True,
            )
            nc.vector.scalar_tensor_tensor(part[i][:, c], y_ps[:], 0.6, nn_row[:, c], ALU.mult, ALU.subtract)

        def affinity(i, c):
            nc.vector.scalar_tensor_tensor(
                arg[i][:, c], part[i][:, c], own_t[:, i : i + 1], loc_ps[:, c], ALU.subtract, ALU.mult
            )
            total = ring.tile([P, 1], F32, name="total", bufs=TILES + 1)
            nc.scalar.activation(aff[i][:, c], arg[i][:, c], ACT.Exp, scale=iloc_t[:, i : i + 1], accum_out=total[:])
            return total

        def hundredth_degree(total):
            hundredth = ring.tile([P, 1], F32, name="divisor")
            nc.scalar.activation(hundredth[:], total[:], ACT.Copy, scale=0.01, bias=0.005)
            return hundredth

        def invert(divisor):
            inv = ring.tile([P, 1], F32, name="inv")
            nc.vector.reciprocal(inv[:], divisor[:])
            return inv

        def store(i, c):
            nc.sync.dma_start(out=out[i * P : (i + 1) * P, c], in_=res[i][:, c])

        for c in halves:
            product(0, c)
        product(1, whole)
        hundredth0 = hundredth_degree(affinity(0, whole))
        product(2, whole)
        hundredth1 = hundredth_degree(affinity(1, whole))
        nc.scalar.activation(res[0][:], aff[0][:], ACT.Copy, scale=invert(hundredth0)[:])
        store(0, whole)
        product(3, halves[0])
        total2 = affinity(2, whole)
        product(3, halves[1])
        inv1 = invert(hundredth1)
        totals3 = [affinity(3, c) for c in halves]
        hundredth2 = ring.tile([P, 1], F32, name="divisor")
        nc.vector.tensor_scalar(hundredth2[:], total2[:], 0.01, 0.005, ALU.mult, ALU.add)
        nc.vector.tensor_scalar(res[1][:], aff[1][:], inv1[:], None, ALU.mult)
        store(1, whole)
        nc.vector.tensor_scalar(res[2][:], aff[2][:], invert(hundredth2)[:], None, ALU.mult)
        store(2, whole)
        deg3 = ring.tile([P, 1], F32, name="divisor")
        nc.vector.tensor_scalar(deg3[:], totals3[0][:], totals3[1][:], 0.5, ALU.add, ALU.add)
        inv3 = invert(deg3)
        for c in halves:
            nc.vector.tensor_scalar(res[3][:, c], aff[3][:, c], inv3[:], 100.0, ALU.mult, ALU.mult)
            store(3, c)
